import numpy as np
import ml_dtypes


def mxq(x, axis, fmt="e4m3"):
    dtype, down = {"e4m3": (ml_dtypes.float8_e4m3fn, 7), "e5m2": (ml_dtypes.float8_e5m2, 14)}[fmt]
    v = np.moveaxis(np.asarray(x, np.float32).astype(ml_dtypes.bfloat16).astype(np.float64), axis, -1)
    blocks = v.reshape(v.shape[:-1] + (-1, 32))
    amax = np.abs(blocks).max(-1, keepdims=True)
    byte = np.maximum(np.where(amax > 0, np.frexp(amax)[1] - 1 + 127, 0) - down, 1)
    scale = np.exp2(byte - 127.0)
    codes = (blocks / scale).astype(np.float32).astype(dtype).astype(np.float64)
    return np.moveaxis((codes * scale).reshape(v.shape), -1, axis)


WIDE = False


def mx_kscale(k):
    if not WIDE:
        return np.ones(k)
    levels = np.array([10, -10, 5, -5, 0])
    if k % 512:
        return np.exp2(np.random.permutation(np.resize(levels, k // 32))).repeat(32)
    a = np.empty((k // 512, 16))
    for p in range(k // 512):
        a[p, :8] = np.random.permutation(np.resize(levels, 8))
        for g in range(8):
            far = levels[np.abs(levels - a[p, g]) >= 10]
            a[p, g + 8] = far[np.random.randint(len(far))]
    return np.exp2(a.ravel()).repeat(32)


def f64(x):
    return np.asarray(x).astype(np.float64)


def striped8(idx):
    return np.concatenate([x.reshape(-1, 16).T for x in idx]).astype(np.uint16)


def runs(offs, k):
    lists = np.stack([offs[16 * r : 16 * r + 16].T.reshape(-1) for r in range(8)]).astype(np.int64)
    return lists[np.arange(k) % 512 // 64]


def pack_weight(w):
    k, n = w.shape
    w = f64(np.asarray(w, np.float32).astype(ml_dtypes.bfloat16)).reshape(k // 32, 32, n)
    amax = np.abs(w).max(1)
    byte = np.clip(np.where(amax > 0, np.frexp(amax)[1] - 1 + 127 - 7, 1), 1, 254)
    scaled = (w * np.exp2(127.0 - byte)[:, None, :]).reshape(k, n).astype(np.float32)
    words = np.ascontiguousarray(scaled.reshape(k // 512, 128, 4, n).transpose(0, 1, 3, 2)).astype(ml_dtypes.float8_e4m3fn).view(np.uint8)
    return words, np.ascontiguousarray(byte.astype(np.uint8).reshape(k // 512, 16, n))


def unpack_weight(words, scales):
    g, p, n, _ = words.shape
    vals = np.ascontiguousarray(words).view(ml_dtypes.float8_e4m3fn).astype(np.float64) * np.repeat(np.exp2(scales.astype(np.float64) - 127.0), 8, axis=1)[..., None]
    return vals.transpose(0, 1, 3, 2).reshape(g * 512, n)


K, T, S, N = 512, 2048, 512, 256


def setup_inputs():
    n = np.random.standard_normal
    s = mx_kscale(K)[:, None]
    packed_xT = pack_weight(n((K, T)) * s)
    return {
        "x_words": packed_xT[0],
        "x_scales": packed_xT[1],
        "w1": (n((K, N)) / np.sqrt(K) / s).astype(np.float32),
        "w2": (n((K, N)) / np.sqrt(K) / s).astype(np.float32),
        "offs": striped8(np.stack([np.random.permutation(T)[:S] for _ in range(8)])),
        "old": striped8(np.stack([np.random.permutation(T)[:S] for _ in range(8)])),
    }


def reference(x_words, x_scales, w1, w2, offs, old):
    xq = unpack_weight(x_words, x_scales)[np.arange(K)[:, None], runs(offs, K)]
    y = mxq(f64(w1), 0, "e4m3").T @ xq
    xold = unpack_weight(x_words, x_scales)[np.arange(K)[:, None], runs(old, K)]
    e = mxq(f64(w2), 0, "e4m3").T @ xold
    return np.abs(y - e)

@@ -1,0 +1,97 @@
+from contextlib import ExitStack
+
+import concourse.mybir as mybir
+
+K, T, S, N = 512, 2048, 512, 256
+FLOPS = 2 * 2 * K * N * S
+
+F32 = mybir.dt.float32
+BF16 = mybir.dt.bfloat16
+I32 = mybir.dt.int32
+U32 = mybir.dt.uint32
+U16 = mybir.dt.uint16
+U8 = mybir.dt.uint8
+FP8X4 = mybir.dt.float8_e4m3fn_x4
+ACT = mybir.ActivationFunctionType
+ALU = mybir.AluOpType
+
+P = 128
+PACK = 4
+M_TILE = 128
+J_TILE = 256
+
+
+def tile_picked_phdiff_abs_p_kernel(tc, x_words, x_scales, w1, w2, offs, old, out):
+    nc = tc.nc
+    with ExitStack() as ctx:
+        keep = ctx.enter_context(tc.tile_pool(name="keep", bufs=1))
+        psum = ctx.enter_context(tc.psum_pool(name="psum", bufs=1))
+
+        lists = []
+        for name, source in (("offs", offs), ("old", old)):
+            list_tile = keep.tile([P, S // 16], U16, name="list_" + name)
+            nc.sync.dma_start(list_tile[:], source)
+            lists.append(list_tile)
+
+        scale_table = keep.tile([P, T], U8, name="scale_table", align_bytes=64)
+        nc.vector.memset(scale_table[:].bitcast(I32), 0)
+        scale_rows = x_scales[0].bitcast(I32)
+        for parity in range(2):
+            nc.sync.dma_start(scale_table[parity:P:16, :].bitcast(I32), scale_rows[parity:16:2, :])
+
+        word_table = keep.tile([P, T], I32, name="word_table", align_bytes=64)
+        raw = [keep.tile([P, PACK, N], F32, name="raw_w%d" % side) for side in range(2)]
+        nc.sync.dma_start(raw[0][:], w1.rearrange("(p t) m -> p t m", t=PACK))
+        nc.sync.dma_start(word_table[:], x_words[0].rearrange("p n t -> p (n t)").bitcast(I32))
+        nc.sync.dma_start(raw[1][:], w2.rearrange("(p t) m -> p t m", t=PACK))
+
+        x_planes = []
+        for side in range(2):
+            picked_scales = keep.tile([P, S], U8, name="picked_scales%d" % side, align_bytes=64)
+            nc.vector.tensor_copy(picked_scales[:], scale_table[:].indirect(lists[side][:]))
+            plane = keep.tile([P, S], U8, name="x_plane%d" % side, align_bytes=64)
+            nc.vector.tensor_copy(plane[:].bitcast(I32), picked_scales[:].bitcast(I32))
+            for row in range(2):
+                nc.sync.dma_start(plane[2 + row : P : 32, :].bitcast(I32), picked_scales[16 + row : P : 32, :].bitcast(I32))
+            x_planes.append(plane)
+
+        picked_words = {}
+        for side in range(2):
+            for jt in range(S // J_TILE):
+                words = keep.tile([P, J_TILE], U32, name="picked_words%d_%d" % (side, jt), align_bytes=64)
+                offsets = lists[side][:, jt * J_TILE // 16 : (jt + 1) * J_TILE // 16]
+                nc.vector.tensor_copy(words[:], word_table[:].bitcast(U32).indirect(offsets))
+                picked_words[side, jt] = words
+
+        w_codes, w_planes = {}, {}
+        for side in range(2):
+            for mt in range(N // M_TILE):
+                grouped = keep.tile([P, M_TILE, PACK], BF16, name="grouped%d_%d" % (side, mt), align_bytes=64)
+                src = raw[side][:, :, mt * M_TILE : (mt + 1) * M_TILE].rearrange("p t (c i) -> p c t i", i=4)
+                dst = grouped[:].rearrange("p (c i) t -> p c t i", i=4)
+                if side == 0:
+                    nc.scalar.copy(dst, src)
+                else:
+                    nc.scalar.activation(dst, src, ACT.Copy, scale=-1.0)
+                codes = keep.tile([P, M_TILE], U32, name="w_codes%d_%d" % (side, mt), align_bytes=64)
+                plane = keep.tile([P, M_TILE], U8, name="w_plane%d_%d" % (side, mt), align_bytes=64)
+                nc.vector.quantize_mx(codes[:].bitcast(FP8X4), plane[:], grouped[:].rearrange("p m t -> p (m t)"))
+                w_codes[side, mt], w_planes[side, mt] = codes, plane
+
+        blocks = [(mt, jt) for mt in range(N // M_TILE) for jt in range(S // J_TILE)]
+        acc = {block: psum.tile([P, J_TILE], F32, name="acc%d_%d" % block) for block in blocks}
+        for side in range(2):
+            for mt, jt in sorted(blocks, key=lambda b: b[::-1]) if side == 0 else blocks:
+                nc.tensor.matmul_mx(
+                    acc[mt, jt][:],
+                    lhsT=w_codes[side, mt][:].bitcast(FP8X4),
+                    lhsT_scale=w_planes[side, mt][:],
+                    rhs=picked_words[side, jt][:].bitcast(FP8X4),
+                    rhs_scale=x_planes[side][:, jt * J_TILE : (jt + 1) * J_TILE],
+                    start=(side == 0),
+                    stop=(side == 1),
+                )
+        for mt, jt in blocks:
+            result = keep.tile([P, J_TILE], F32, name="result%d_%d" % (mt, jt))
+            nc.scalar.activation(result[:], acc[mt, jt][:], ACT.Abs)
+            nc.sync.dma_start(out[mt * M_TILE : (mt + 1) * M_TILE, jt * J_TILE : (jt + 1) * J_TILE], result[:])

@@ -27,11 +27,9 @@ def tile_picked_phdiff_abs_p_kernel(tc, x_words, x_scales, w1, w2, offs, old, ou
         keep = ctx.enter_context(tc.tile_pool(name="keep", bufs=1))
         psum = ctx.enter_context(tc.psum_pool(name="psum", bufs=1))
 
-        lists = []
-        for name, source in (("offs", offs), ("old", old)):
-            list_tile = keep.tile([P, S // 16], U16, name="list_" + name)
-            nc.sync.dma_start(list_tile[:], source)
-            lists.append(list_tile)
+        lists = [keep.tile([P, S // 16], U16, name="list%d" % side) for side in range(2)]
+        nc.sync.dma_start(lists[0][:], offs)
+        nc.sync.dma_start(lists[1][:], old)
 
         scale_table = keep.tile([P, T], U8, name="scale_table", align_bytes=64)
         nc.vector.memset(scale_table[:].bitcast(I32), 0)
@@ -41,7 +39,7 @@ def tile_picked_phdiff_abs_p_kernel(tc, x_words, x_scales, w1, w2, offs, old, ou
 
         word_table = keep.tile([P, T], I32, name="word_table", align_bytes=64)
         raw = [keep.tile([P, PACK, N], F32, name="raw_w%d" % side) for side in range(2)]
-        nc.sync.dma_start(raw[0][:], w1.rearrange("(p t) m -> p t m", t=PACK))
+        nc.scalar.dma_start(raw[0][:], w1.rearrange("(p t) m -> p t m", t=PACK))
         nc.sync.dma_start(word_table[:], x_words[0].rearrange("p n t -> p (n t)").bitcast(I32))
         nc.sync.dma_start(raw[1][:], w2.rearrange("(p t) m -> p t m", t=PACK))
 
@@ -50,38 +48,46 @@ def tile_picked_phdiff_abs_p_kernel(tc, x_words, x_scales, w1, w2, offs, old, ou
             picked_scales = keep.tile([P, S], U8, name="picked_scales%d" % side, align_bytes=64)
             nc.vector.tensor_copy(picked_scales[:], scale_table[:].indirect(lists[side][:]))
             plane = keep.tile([P, S], U8, name="x_plane%d" % side, align_bytes=64)
-            nc.vector.tensor_copy(plane[:].bitcast(I32), picked_scales[:].bitcast(I32))
-            for row in range(2):
-                nc.sync.dma_start(plane[2 + row : P : 32, :].bitcast(I32), picked_scales[16 + row : P : 32, :].bitcast(I32))
+            if side == 0:
+                nc.vector.memset(plane[:].bitcast(I32), 0)
+            else:
+                nc.vector.tensor_copy(plane[:].bitcast(I32), picked_scales[:].bitcast(I32))
+            for row in range(2 * side, 4):
+                first = 16 * (row // 2) + row % 2
+                nc.sync.dma_start(plane[row:P:32, :].bitcast(I32), picked_scales[first:P:32, :].bitcast(I32))
             x_planes.append(plane)
 
-        picked_words = {}
-        for side in range(2):
-            for jt in range(S // J_TILE):
-                words = keep.tile([P, J_TILE], U32, name="picked_words%d_%d" % (side, jt), align_bytes=64)
-                offsets = lists[side][:, jt * J_TILE // 16 : (jt + 1) * J_TILE // 16]
-                nc.vector.tensor_copy(words[:], word_table[:].bitcast(U32).indirect(offsets))
-                picked_words[side, jt] = words
+        picked_words, w_codes, w_planes = {}, {}, {}
 
-        w_codes, w_planes = {}, {}
-        for side in range(2):
-            for mt in range(N // M_TILE):
-                grouped = keep.tile([P, M_TILE, PACK], BF16, name="grouped%d_%d" % (side, mt), align_bytes=64)
-                src = raw[side][:, :, mt * M_TILE : (mt + 1) * M_TILE].rearrange("p t (c i) -> p c t i", i=4)
-                dst = grouped[:].rearrange("p (c i) t -> p c t i", i=4)
-                if side == 0:
-                    nc.scalar.copy(dst, src)
-                else:
-                    nc.scalar.activation(dst, src, ACT.Copy, scale=-1.0)
-                codes = keep.tile([P, M_TILE], U32, name="w_codes%d_%d" % (side, mt), align_bytes=64)
-                plane = keep.tile([P, M_TILE], U8, name="w_plane%d_%d" % (side, mt), align_bytes=64)
-                nc.vector.quantize_mx(codes[:].bitcast(FP8X4), plane[:], grouped[:].rearrange("p m t -> p (m t)"))
-                w_codes[side, mt], w_planes[side, mt] = codes, plane
+        def gather_words(side, jt, tag):
+            words = keep.tile([P, J_TILE], U32, name="picked_words%d_%d" % (side, jt), tag=tag, align_bytes=64)
+            offsets = lists[side][:, jt * J_TILE // 16 : (jt + 1) * J_TILE // 16]
+            nc.vector.tensor_copy(words[:], word_table[:].bitcast(U32).indirect(offsets))
+            picked_words[side, jt] = words
+
+        def quantise_weights(side, mt):
+            grouped = keep.tile([P, M_TILE, PACK], BF16, name="grouped%d_%d" % (side, mt), tag="grouped%d_%d" % (side, mt), align_bytes=64)
+            src = raw[side][:, :, mt * M_TILE : (mt + 1) * M_TILE].rearrange("p t (c i) -> p c t i", i=4)
+            dst = grouped[:].rearrange("p (c i) t -> p c t i", i=4)
+            nc.scalar.activation(dst, src, ACT.Copy, scale=1.0 if side == 0 else -1.0)
+            codes = keep.tile([P, M_TILE], U32, name="w_codes%d_%d" % (side, mt), align_bytes=64)
+            plane = keep.tile([P, M_TILE], U8, name="w_plane%d_%d" % (side, mt), align_bytes=64)
+            nc.vector.quantize_mx(codes[:].bitcast(FP8X4), plane[:], grouped[:].rearrange("p m t -> p (m t)"))
+            w_codes[side, mt], w_planes[side, mt] = codes, plane
+
+        quantise_weights(0, 0)
+        quantise_weights(0, 1)
+        gather_words(0, 0, "words0_0")
+        gather_words(0, 1, "words0_1")
+        gather_words(1, 0, "words1_0")
+        quantise_weights(1, 0)
+        gather_words(1, 1, "grouped1_0")
+        quantise_weights(1, 1)
 
         blocks = [(mt, jt) for mt in range(N // M_TILE) for jt in range(S // J_TILE)]
         acc = {block: psum.tile([P, J_TILE], F32, name="acc%d_%d" % block) for block in blocks}
         for side in range(2):
-            for mt, jt in sorted(blocks, key=lambda b: b[::-1]) if side == 0 else blocks:
+            for mt, jt in blocks:
                 nc.tensor.matmul_mx(
                     acc[mt, jt][:],
                     lhsT=w_codes[side, mt][:].bitcast(FP8X4),

@@ -19,6 +19,7 @@ P = 128
 PACK = 4
 M_TILE = 128
 J_TILE = 256
+EARLY = 256
 
 
 def tile_picked_phdiff_abs_p_kernel(tc, x_words, x_scales, w1, w2, offs, old, out):
@@ -29,18 +30,18 @@ def tile_picked_phdiff_abs_p_kernel(tc, x_words, x_scales, w1, w2, offs, old, ou
 
         lists = [keep.tile([P, S // 16], U16, name="list%d" % side) for side in range(2)]
         nc.sync.dma_start(lists[0][:], offs)
+        word_table = keep.tile([P, T], I32, name="word_table", align_bytes=64)
+        word_rows = x_words[0].rearrange("p n t -> p (n t)").bitcast(I32)
+        nc.sync.dma_start(word_table[:, :EARLY], word_rows[:, :EARLY])
         nc.sync.dma_start(lists[1][:], old)
 
         scale_table = keep.tile([P, T], U8, name="scale_table", align_bytes=64)
         nc.vector.memset(scale_table[:].bitcast(I32), 0)
-        scale_rows = x_scales[0].bitcast(I32)
-        for parity in range(2):
-            nc.sync.dma_start(scale_table[parity:P:16, :].bitcast(I32), scale_rows[parity:16:2, :])
+        nc.sync.dma_start(scale_table[0:P:8, :].bitcast(I32), x_scales[0].bitcast(I32))
 
-        word_table = keep.tile([P, T], I32, name="word_table", align_bytes=64)
         raw = [keep.tile([P, PACK, N], F32, name="raw_w%d" % side) for side in range(2)]
-        nc.scalar.dma_start(raw[0][:], w1.rearrange("(p t) m -> p t m", t=PACK))
-        nc.sync.dma_start(word_table[:], x_words[0].rearrange("p n t -> p (n t)").bitcast(I32))
+        nc.sync.dma_start(raw[0][:], w1.rearrange("(p t) m -> p t m", t=PACK))
+        nc.sync.dma_start(word_table[:, EARLY:], word_rows[:, EARLY:])
         nc.sync.dma_start(raw[1][:], w2.rearrange("(p t) m -> p t m", t=PACK))
 
         x_planes = []
@@ -52,37 +53,37 @@ def tile_picked_phdiff_abs_p_kernel(tc, x_words, x_scales, w1, w2, offs, old, ou
                 nc.vector.memset(plane[:].bitcast(I32), 0)
             else:
                 nc.vector.tensor_copy(plane[:].bitcast(I32), picked_scales[:].bitcast(I32))
-            for row in range(2 * side, 4):
-                first = 16 * (row // 2) + row % 2
-                nc.sync.dma_start(plane[row:P:32, :].bitcast(I32), picked_scales[first:P:32, :].bitcast(I32))
+            for row in range(side, 4):
+                nc.sync.dma_start(plane[row:P:32, :].bitcast(I32), picked_scales[8 * row : P : 32, :].bitcast(I32))
             x_planes.append(plane)
 
         picked_words, w_codes, w_planes = {}, {}, {}
 
-        def gather_words(side, jt, tag):
-            words = keep.tile([P, J_TILE], U32, name="picked_words%d_%d" % (side, jt), tag=tag, align_bytes=64)
-            offsets = lists[side][:, jt * J_TILE // 16 : (jt + 1) * J_TILE // 16]
-            nc.vector.tensor_copy(words[:], word_table[:].bitcast(U32).indirect(offsets))
-            picked_words[side, jt] = words
+        def gather_words(pieces, tag):
+            words = keep.tile([P, len(pieces), J_TILE], U32, name="picked_" + tag, tag=tag, align_bytes=64)
+            for place, (side, jt) in enumerate(pieces):
+                offsets = lists[side][:, jt * J_TILE // 16 : (jt + 1) * J_TILE // 16]
+                nc.vector.tensor_copy(words[:, place, :], word_table[:].bitcast(U32).indirect(offsets))
+                picked_words[side, jt] = words[:, place, :]
 
-        def quantise_weights(side, mt):
-            grouped = keep.tile([P, M_TILE, PACK], BF16, name="grouped%d_%d" % (side, mt), tag="grouped%d_%d" % (side, mt), align_bytes=64)
-            src = raw[side][:, :, mt * M_TILE : (mt + 1) * M_TILE].rearrange("p t (c i) -> p c t i", i=4)
+        def quantise_weights(side, m_tiles, tag):
+            first, width = m_tiles[0] * M_TILE, len(m_tiles) * M_TILE
+            grouped = keep.tile([P, width, PACK], BF16, name="grouped_" + tag, tag=tag, align_bytes=64)
+            src = raw[side][:, :, first : first + width].rearrange("p t (c i) -> p c t i", i=4)
             dst = grouped[:].rearrange("p (c i) t -> p c t i", i=4)
             nc.scalar.activation(dst, src, ACT.Copy, scale=1.0 if side == 0 else -1.0)
-            codes = keep.tile([P, M_TILE], U32, name="w_codes%d_%d" % (side, mt), align_bytes=64)
-            plane = keep.tile([P, M_TILE], U8, name="w_plane%d_%d" % (side, mt), align_bytes=64)
+            codes = keep.tile([P, width], U32, name="w_codes_" + tag, align_bytes=64)
+            plane = keep.tile([P, width], U8, name="w_plane_" + tag, align_bytes=64)
             nc.vector.quantize_mx(codes[:].bitcast(FP8X4), plane[:], grouped[:].rearrange("p m t -> p (m t)"))
-            w_codes[side, mt], w_planes[side, mt] = codes, plane
+            for place, mt in enumerate(m_tiles):
+                w_codes[side, mt] = codes[:, place * M_TILE : (place + 1) * M_TILE]
+                w_planes[side, mt] = plane[:, place * M_TILE : (place + 1) * M_TILE]
 
-        quantise_weights(0, 0)
-        quantise_weights(0, 1)
-        gather_words(0, 0, "words0_0")
-        gather_words(0, 1, "words0_1")
-        gather_words(1, 0, "words1_0")
-        quantise_weights(1, 0)
-        gather_words(1, 1, "grouped1_0")
-        quantise_weights(1, 1)
+        quantise_weights(0, [0, 1], "slot_a")
+        gather_words([(0, 0), (0, 1), (1, 0)], "slot_a")
+        quantise_weights(1, [0], "slot_b")
+        gather_words([(1, 1)], "slot_b")
+        quantise_weights(1, [1], "slot_c")
 
         blocks = [(mt, jt) for mt in range(N // M_TILE) for jt in range(S // J_TILE)]
         acc = {block: psum.tile([P, J_TILE], F32, name="acc%d_%d" % block) for block in blocks}
@@ -90,9 +91,9 @@ def tile_picked_phdiff_abs_p_kernel(tc, x_words, x_scales, w1, w2, offs, old, ou
             for mt, jt in blocks:
                 nc.tensor.matmul_mx(
                     acc[mt, jt][:],
-                    lhsT=w_codes[side, mt][:].bitcast(FP8X4),
-                    lhsT_scale=w_planes[side, mt][:],
-                    rhs=picked_words[side, jt][:].bitcast(FP8X4),
+                    lhsT=w_codes[side, mt].bitcast(FP8X4),
+                    lhsT_scale=w_planes[side, mt],
+                    rhs=picked_words[side, jt].bitcast(FP8X4),
                     rhs_scale=x_planes[side][:, jt * J_TILE : (jt + 1) * J_TILE],
                     start=(side == 0),
                     stop=(side == 1),

@@ -13,10 +13,13 @@ U16 = mybir.dt.uint16
 U8 = mybir.dt.uint8
 FP8X4 = mybir.dt.float8_e4m3fn_x4
 ACT = mybir.ActivationFunctionType
-ALU = mybir.AluOpType
 
 P = 128
 PACK = 4
+LIST_ROWS = 16
+BLOCK_ROWS = 8
+QUADRANT = 32
+LINE = 4
 M_TILE = 128
 J_TILE = 256
 EARLY = 256
@@ -28,7 +31,7 @@ def tile_picked_phdiff_abs_p_kernel(tc, x_words, x_scales, w1, w2, offs, old, ou
         keep = ctx.enter_context(tc.tile_pool(name="keep", bufs=1))
         psum = ctx.enter_context(tc.psum_pool(name="psum", bufs=1))
 
-        lists = [keep.tile([P, S // 16], U16, name="list%d" % side) for side in range(2)]
+        lists = [keep.tile([P, S // LIST_ROWS], U16, name="list%d" % side) for side in range(2)]
         nc.sync.dma_start(lists[0][:], offs)
         word_table = keep.tile([P, T], I32, name="word_table", align_bytes=64)
         word_rows = x_words[0].rearrange("p n t -> p (n t)").bitcast(I32)
@@ -37,58 +40,63 @@ def tile_picked_phdiff_abs_p_kernel(tc, x_words, x_scales, w1, w2, offs, old, ou
 
         scale_table = keep.tile([P, T], U8, name="scale_table", align_bytes=64)
         nc.vector.memset(scale_table[:].bitcast(I32), 0)
-        nc.sync.dma_start(scale_table[0:P:8, :].bitcast(I32), x_scales[0].bitcast(I32))
+        nc.sync.dma_start(scale_table[0:P:BLOCK_ROWS, :].bitcast(I32), x_scales[0].bitcast(I32))
 
-        raw = [keep.tile([P, PACK, N], F32, name="raw_w%d" % side) for side in range(2)]
+        raw = [keep.tile([P, PACK, N], F32, name="raw_w%d" % side, tag="raw_w%d" % side, align_bytes=64) for side in range(2)]
         nc.sync.dma_start(raw[0][:], w1.rearrange("(p t) m -> p t m", t=PACK))
         nc.sync.dma_start(word_table[:, EARLY:], word_rows[:, EARLY:])
         nc.sync.dma_start(raw[1][:], w2.rearrange("(p t) m -> p t m", t=PACK))
 
-        x_planes = []
-        for side in range(2):
-            picked_scales = keep.tile([P, S], U8, name="picked_scales%d" % side, align_bytes=64)
-            nc.vector.tensor_copy(picked_scales[:], scale_table[:].indirect(lists[side][:]))
-            plane = keep.tile([P, S], U8, name="x_plane%d" % side, align_bytes=64)
-            if side == 0:
-                nc.vector.memset(plane[:].bitcast(I32), 0)
-            else:
-                nc.vector.tensor_copy(plane[:].bitcast(I32), picked_scales[:].bitcast(I32))
-            for row in range(side, 4):
-                nc.sync.dma_start(plane[row:P:32, :].bitcast(I32), picked_scales[8 * row : P : 32, :].bitcast(I32))
-            x_planes.append(plane)
+        picked_scales = [keep.tile([P, S], U8, name="picked_scales%d" % side, align_bytes=64) for side in range(2)]
+        x_planes, picked_words, w_codes, w_planes = {}, {}, {}, {}
 
-        picked_words, w_codes, w_planes = {}, {}, {}
+        def move_scale_rows(side, places):
+            for i in places:
+                nc.sync.dma_start(
+                    x_planes[side][i:P:QUADRANT, :].bitcast(I32),
+                    picked_scales[side][BLOCK_ROWS * i : P : QUADRANT, :].bitcast(I32),
+                )
 
-        def gather_words(pieces, tag):
-            words = keep.tile([P, len(pieces), J_TILE], U32, name="picked_" + tag, tag=tag, align_bytes=64)
+        def gather_words(pieces, slot):
+            words = keep.tile([P, len(pieces), J_TILE], U32, name="picked_" + slot, tag=slot, align_bytes=64)
             for place, (side, jt) in enumerate(pieces):
-                offsets = lists[side][:, jt * J_TILE // 16 : (jt + 1) * J_TILE // 16]
+                offsets = lists[side][:, jt * J_TILE // LIST_ROWS : (jt + 1) * J_TILE // LIST_ROWS]
                 nc.vector.tensor_copy(words[:, place, :], word_table[:].bitcast(U32).indirect(offsets))
                 picked_words[side, jt] = words[:, place, :]
 
-        def quantise_weights(side, m_tiles, tag):
+        def quantise_weights(side, m_tiles, slot):
             first, width = m_tiles[0] * M_TILE, len(m_tiles) * M_TILE
-            grouped = keep.tile([P, width, PACK], BF16, name="grouped_" + tag, tag=tag, align_bytes=64)
-            src = raw[side][:, :, first : first + width].rearrange("p t (c i) -> p c t i", i=4)
-            dst = grouped[:].rearrange("p (c i) t -> p c t i", i=4)
+            grouped = keep.tile([P, width, PACK], BF16, name="grouped_" + slot, tag=slot, align_bytes=64)
+            src = raw[side][:, :, first : first + width].rearrange("p t (c n) -> p c t n", n=LINE)
+            dst = grouped[:].rearrange("p (c n) t -> p c t n", n=LINE)
             nc.scalar.activation(dst, src, ACT.Copy, scale=1.0 if side == 0 else -1.0)
-            codes = keep.tile([P, width], U32, name="w_codes_" + tag, align_bytes=64)
-            plane = keep.tile([P, width], U8, name="w_plane_" + tag, align_bytes=64)
-            nc.vector.quantize_mx(codes[:].bitcast(FP8X4), plane[:], grouped[:].rearrange("p m t -> p (m t)"))
+            codes = keep.tile([P, width], U32, name="w_codes_" + slot, align_bytes=64)
+            w_plane = keep.tile([P, width], U8, name="w_plane_" + slot, align_bytes=64)
+            nc.vector.quantize_mx(codes[:].bitcast(FP8X4), w_plane[:], grouped[:].rearrange("p m t -> p (m t)"))
             for place, mt in enumerate(m_tiles):
                 w_codes[side, mt] = codes[:, place * M_TILE : (place + 1) * M_TILE]
-                w_planes[side, mt] = plane[:, place * M_TILE : (place + 1) * M_TILE]
+                w_planes[side, mt] = w_plane[:, place * M_TILE : (place + 1) * M_TILE]
 
+        x_planes[0] = keep.tile([P, S], U8, name="x_plane0", align_bytes=64)
+        nc.vector.memset(x_planes[0][:].bitcast(I32), 0)
+        nc.vector.tensor_copy(picked_scales[0][:], scale_table[:].indirect(lists[0][:]))
+        move_scale_rows(0, range(0, 4))
+        nc.vector.tensor_copy(picked_scales[1][:], scale_table[:].indirect(lists[1][:]))
         quantise_weights(0, [0, 1], "slot_a")
+
+        x_planes[1] = keep.tile([P, S], U8, name="x_plane1", tag="raw_w0", align_bytes=64)
+        nc.vector.tensor_copy(x_planes[1][:].bitcast(I32), picked_scales[1][:].bitcast(I32))
+        move_scale_rows(1, range(1, 4))
+
         gather_words([(0, 0), (0, 1), (1, 0)], "slot_a")
         quantise_weights(1, [0], "slot_b")
         gather_words([(1, 1)], "slot_b")
         quantise_weights(1, [1], "slot_c")
 
-        blocks = [(mt, jt) for mt in range(N // M_TILE) for jt in range(S // J_TILE)]
-        acc = {block: psum.tile([P, J_TILE], F32, name="acc%d_%d" % block) for block in blocks}
+        pieces_out = [(mt, jt) for mt in range(N // M_TILE) for jt in range(S // J_TILE)]
+        acc = {piece: psum.tile([P, J_TILE], F32, name="acc%d_%d" % piece) for piece in pieces_out}
         for side in range(2):
-            for mt, jt in blocks:
+            for mt, jt in pieces_out:
                 nc.tensor.matmul_mx(
                     acc[mt, jt][:],
                     lhsT=w_codes[side, mt].bitcast(FP8X4),
@@ -98,7 +106,7 @@ def tile_picked_phdiff_abs_p_kernel(tc, x_words, x_scales, w1, w2, offs, old, ou
                     start=(side == 0),
                     stop=(side == 1),
                 )
-        for mt, jt in blocks:
+        for mt, jt in pieces_out:
             result = keep.tile([P, J_TILE], F32, name="result%d_%d" % (mt, jt))
             nc.scalar.activation(result[:], acc[mt, jt][:], ACT.Abs)
             nc.sync.dma_start(out[mt * M_TILE : (mt + 1) * M_TILE, jt * J_TILE : (jt + 1) * J_TILE], result[:])

@@ -17,7 +17,6 @@ ACT = mybir.ActivationFunctionType
 P = 128
 PACK = 4
 LIST_ROWS = 16
-BLOCK_ROWS = 8
 QUADRANT = 32
 LINE = 4
 M_TILE = 128
@@ -40,12 +39,22 @@ def tile_picked_phdiff_abs_p_kernel(tc, x_words, x_scales, w1, w2, offs, old, ou
 
         scale_table = keep.tile([P, T], U8, name="scale_table", align_bytes=64)
         nc.vector.memset(scale_table[:].bitcast(I32), 0)
-        nc.sync.dma_start(scale_table[0:P:BLOCK_ROWS, :].bitcast(I32), x_scales[0].bitcast(I32))
+        for e in range(2):
+            nc.sync.dma_start(scale_table[e:P:LIST_ROWS, :].bitcast(I32), x_scales[0].bitcast(I32)[e::2, :])
 
-        raw = [keep.tile([P, PACK, N], F32, name="raw_w%d" % side, tag="raw_w%d" % side, align_bytes=64) for side in range(2)]
-        nc.sync.dma_start(raw[0][:], w1.rearrange("(p t) m -> p t m", t=PACK))
+        raw = {}
+
+        def load_weights(side, m_tiles, slot):
+            first, width = m_tiles[0] * M_TILE, len(m_tiles) * M_TILE
+            rows = keep.tile([P, PACK, width], F32, name=slot, tag=slot, align_bytes=64)
+            weights = (w1, w2)[side].rearrange("(p t) m -> p t m", t=PACK)
+            nc.sync.dma_start(rows[:], weights[:, :, first : first + width])
+            raw[side, m_tiles[0]] = rows
+
+        load_weights(0, [0, 1], "raw_w1")
         nc.sync.dma_start(word_table[:, EARLY:], word_rows[:, EARLY:])
-        nc.sync.dma_start(raw[1][:], w2.rearrange("(p t) m -> p t m", t=PACK))
+        load_weights(1, [0], "raw_w2_first")
+        load_weights(1, [1], "raw_w2_second")
 
         picked_scales = [keep.tile([P, S], U8, name="picked_scales%d" % side, align_bytes=64) for side in range(2)]
         x_planes, picked_words, w_codes, w_planes = {}, {}, {}, {}
@@ -54,20 +63,21 @@ def tile_picked_phdiff_abs_p_kernel(tc, x_words, x_scales, w1, w2, offs, old, ou
             for i in places:
                 nc.sync.dma_start(
                     x_planes[side][i:P:QUADRANT, :].bitcast(I32),
-                    picked_scales[side][BLOCK_ROWS * i : P : QUADRANT, :].bitcast(I32),
+                    picked_scales[side][LIST_ROWS * (i // 2) + i % 2 : P : QUADRANT, :].bitcast(I32),
                 )
 
         def gather_words(pieces, slot):
-            words = keep.tile([P, len(pieces), J_TILE], U32, name="picked_" + slot, tag=slot, align_bytes=64)
+            words = keep.tile([P, len(pieces) * J_TILE], U32, name="picked_" + slot, tag=slot, align_bytes=64)
             for place, (side, jt) in enumerate(pieces):
                 offsets = lists[side][:, jt * J_TILE // LIST_ROWS : (jt + 1) * J_TILE // LIST_ROWS]
-                nc.vector.tensor_copy(words[:, place, :], word_table[:].bitcast(U32).indirect(offsets))
-                picked_words[side, jt] = words[:, place, :]
+                piece = words[:, place * J_TILE : (place + 1) * J_TILE]
+                nc.vector.tensor_copy(piece, word_table[:].bitcast(U32).indirect(offsets))
+                picked_words[side, jt] = piece
 
         def quantise_weights(side, m_tiles, slot):
-            first, width = m_tiles[0] * M_TILE, len(m_tiles) * M_TILE
+            width = len(m_tiles) * M_TILE
             grouped = keep.tile([P, width, PACK], BF16, name="grouped_" + slot, tag=slot, align_bytes=64)
-            src = raw[side][:, :, first : first + width].rearrange("p t (c n) -> p c t n", n=LINE)
+            src = raw[side, m_tiles[0]][:].rearrange("p t (c n) -> p c t n", n=LINE)
             dst = grouped[:].rearrange("p (c n) t -> p c t n", n=LINE)
             nc.scalar.activation(dst, src, ACT.Copy, scale=1.0 if side == 0 else -1.0)
             codes = keep.tile([P, width], U32, name="w_codes_" + slot, align_bytes=64)
@@ -84,13 +94,13 @@ def tile_picked_phdiff_abs_p_kernel(tc, x_words, x_scales, w1, w2, offs, old, ou
         nc.vector.tensor_copy(picked_scales[1][:], scale_table[:].indirect(lists[1][:]))
         quantise_weights(0, [0, 1], "slot_a")
 
-        x_planes[1] = keep.tile([P, S], U8, name="x_plane1", tag="raw_w0", align_bytes=64)
+        x_planes[1] = keep.tile([P, S], U8, name="x_plane1", tag="raw_w1", align_bytes=64)
         nc.vector.tensor_copy(x_planes[1][:].bitcast(I32), picked_scales[1][:].bitcast(I32))
-        move_scale_rows(1, range(1, 4))
+        move_scale_rows(1, range(2, 4))
 
         gather_words([(0, 0), (0, 1), (1, 0)], "slot_a")
         quantise_weights(1, [0], "slot_b")
-        gather_words([(1, 1)], "slot_b")
+        gather_words([(1, 1)], "raw_w2_first")
         quantise_weights(1, [1], "slot_c")
 
         pieces_out = [(mt, jt) for mt in range(N // M_TILE) for jt in range(S // J_TILE)]

@@ -28,6 +28,7 @@ def tile_picked_phdiff_abs_p_kernel(tc, x_words, x_scales, w1, w2, offs, old, ou
     nc = tc.nc
     with ExitStack() as ctx:
         keep = ctx.enter_context(tc.tile_pool(name="keep", bufs=1))
+        reuse = ctx.enter_context(tc.tile_pool(name="reuse", bufs=1))
         psum = ctx.enter_context(tc.psum_pool(name="psum", bufs=1))
 
         lists = [keep.tile([P, S // LIST_ROWS], U16, name="list%d" % side) for side in range(2)]
@@ -39,22 +40,20 @@ def tile_picked_phdiff_abs_p_kernel(tc, x_words, x_scales, w1, w2, offs, old, ou
 
         scale_table = keep.tile([P, T], U8, name="scale_table", align_bytes=64)
         nc.vector.memset(scale_table[:].bitcast(I32), 0)
-        for e in range(2):
-            nc.sync.dma_start(scale_table[e:P:LIST_ROWS, :].bitcast(I32), x_scales[0].bitcast(I32)[e::2, :])
+        for e, queue in enumerate((nc.sync, nc.scalar)):
+            queue.dma_start(scale_table[e:P:LIST_ROWS, :].bitcast(I32), x_scales[0].bitcast(I32)[e::2, :])
 
         raw = {}
 
-        def load_weights(side, m_tiles, slot):
+        def load_weights(side, m_tiles, rows):
             first, width = m_tiles[0] * M_TILE, len(m_tiles) * M_TILE
-            rows = keep.tile([P, PACK, width], F32, name=slot, tag=slot, align_bytes=64)
             weights = (w1, w2)[side].rearrange("(p t) m -> p t m", t=PACK)
             nc.sync.dma_start(rows[:], weights[:, :, first : first + width])
             raw[side, m_tiles[0]] = rows
 
-        load_weights(0, [0, 1], "raw_w1")
+        load_weights(0, [0, 1], reuse.tile([P, PACK, N], F32, name="raw_w1", align_bytes=64, offset=0))
         nc.sync.dma_start(word_table[:, EARLY:], word_rows[:, EARLY:])
-        load_weights(1, [0], "raw_w2_first")
-        load_weights(1, [1], "raw_w2_second")
+        load_weights(1, [0], keep.tile([P, PACK, M_TILE], F32, name="raw_w2_first", tag="raw_w2_first", align_bytes=64))
 
         picked_scales = [keep.tile([P, S], U8, name="picked_scales%d" % side, align_bytes=64) for side in range(2)]
         x_planes, picked_words, w_codes, w_planes = {}, {}, {}, {}
@@ -93,8 +92,9 @@ def tile_picked_phdiff_abs_p_kernel(tc, x_words, x_scales, w1, w2, offs, old, ou
         move_scale_rows(0, range(0, 4))
         nc.vector.tensor_copy(picked_scales[1][:], scale_table[:].indirect(lists[1][:]))
         quantise_weights(0, [0, 1], "slot_a")
+        load_weights(1, [1], reuse.tile([P, PACK, M_TILE], F32, name="raw_w2_second", align_bytes=64, offset=2048))
 
-        x_planes[1] = keep.tile([P, S], U8, name="x_plane1", tag="raw_w1", align_bytes=64)
+        x_planes[1] = reuse.tile([P, S], U8, name="x_plane1", align_bytes=64, offset=0)
         nc.vector.tensor_copy(x_planes[1][:].bitcast(I32), picked_scales[1][:].bitcast(I32))
         move_scale_rows(1, range(2, 4))
 

@@ -21,7 +21,7 @@ QUADRANT = 32
 LINE = 4
 M_TILE = 128
 J_TILE = 256
-EARLY = 256
+EARLY = 384
 
 
 def tile_picked_phdiff_abs_p_kernel(tc, x_words, x_scales, w1, w2, offs, old, out):
@@ -32,10 +32,10 @@ def tile_picked_phdiff_abs_p_kernel(tc, x_words, x_scales, w1, w2, offs, old, ou
         psum = ctx.enter_context(tc.psum_pool(name="psum", bufs=1))
 
         lists = [keep.tile([P, S // LIST_ROWS], U16, name="list%d" % side) for side in range(2)]
-        nc.sync.dma_start(lists[0][:], offs)
         word_table = keep.tile([P, T], I32, name="word_table", align_bytes=64)
         word_rows = x_words[0].rearrange("p n t -> p (n t)").bitcast(I32)
         nc.sync.dma_start(word_table[:, :EARLY], word_rows[:, :EARLY])
+        nc.sync.dma_start(lists[0][:], offs)
         nc.sync.dma_start(lists[1][:], old)
 
         scale_table = keep.tile([P, T], U8, name="scale_table", align_bytes=64)
@@ -105,8 +105,9 @@ def tile_picked_phdiff_abs_p_kernel(tc, x_words, x_scales, w1, w2, offs, old, ou
 
         pieces_out = [(mt, jt) for mt in range(N // M_TILE) for jt in range(S // J_TILE)]
         acc = {piece: psum.tile([P, J_TILE], F32, name="acc%d_%d" % piece) for piece in pieces_out}
+        by_columns = sorted(pieces_out, key=lambda piece: piece[1])
         for side in range(2):
-            for mt, jt in pieces_out:
+            for mt, jt in (by_columns, pieces_out)[side]:
                 nc.tensor.matmul_mx(
                     acc[mt, jt][:],
                     lhsT=w_codes[side, mt].bitcast(FP8X4),

@@ -17,7 +17,9 @@ ACT = mybir.ActivationFunctionType
 P = 128
 PACK = 4
 LIST_ROWS = 16
+BLOCK_ROWS = 8
 QUADRANT = 32
+PLACES = 4
 LINE = 4
 M_TILE = 128
 J_TILE = 256
@@ -28,7 +30,6 @@ def tile_picked_phdiff_abs_p_kernel(tc, x_words, x_scales, w1, w2, offs, old, ou
     nc = tc.nc
     with ExitStack() as ctx:
         keep = ctx.enter_context(tc.tile_pool(name="keep", bufs=1))
-        reuse = ctx.enter_context(tc.tile_pool(name="reuse", bufs=1))
         psum = ctx.enter_context(tc.psum_pool(name="psum", bufs=1))
 
         lists = [keep.tile([P, S // LIST_ROWS], U16, name="list%d" % side) for side in range(2)]
@@ -38,10 +39,9 @@ def tile_picked_phdiff_abs_p_kernel(tc, x_words, x_scales, w1, w2, offs, old, ou
         nc.sync.dma_start(lists[0][:], offs)
         nc.sync.dma_start(lists[1][:], old)
 
-        scale_table = keep.tile([P, T], U8, name="scale_table", align_bytes=64)
+        scale_table = keep.tile([P, T], U8, name="scale_table", tag="scale_table", align_bytes=64)
         nc.vector.memset(scale_table[:].bitcast(I32), 0)
-        for e, queue in enumerate((nc.sync, nc.scalar)):
-            queue.dma_start(scale_table[e:P:LIST_ROWS, :].bitcast(I32), x_scales[0].bitcast(I32)[e::2, :])
+        nc.sync.dma_start(scale_table[0:P:BLOCK_ROWS, :].bitcast(I32), x_scales[0].bitcast(I32))
 
         raw = {}
 
@@ -51,18 +51,18 @@ def tile_picked_phdiff_abs_p_kernel(tc, x_words, x_scales, w1, w2, offs, old, ou
             nc.sync.dma_start(rows[:], weights[:, :, first : first + width])
             raw[side, m_tiles[0]] = rows
 
-        load_weights(0, [0, 1], reuse.tile([P, PACK, N], F32, name="raw_w1", align_bytes=64, offset=0))
+        load_weights(0, [0, 1], keep.tile([P, PACK, N], F32, name="raw_w1", align_bytes=64))
         nc.sync.dma_start(word_table[:, EARLY:], word_rows[:, EARLY:])
         load_weights(1, [0], keep.tile([P, PACK, M_TILE], F32, name="raw_w2_first", tag="raw_w2_first", align_bytes=64))
 
         picked_scales = [keep.tile([P, S], U8, name="picked_scales%d" % side, align_bytes=64) for side in range(2)]
         x_planes, picked_words, w_codes, w_planes = {}, {}, {}, {}
 
-        def move_scale_rows(side, places):
-            for i in places:
+        def move_scale_rows(side):
+            for i in range(PLACES):
                 nc.sync.dma_start(
                     x_planes[side][i:P:QUADRANT, :].bitcast(I32),
-                    picked_scales[side][LIST_ROWS * (i // 2) + i % 2 : P : QUADRANT, :].bitcast(I32),
+                    picked_scales[side][BLOCK_ROWS * i : P : QUADRANT, :].bitcast(I32),
                 )
 
         def gather_words(pieces, slot):
@@ -82,32 +82,31 @@ def tile_picked_phdiff_abs_p_kernel(tc, x_words, x_scales, w1, w2, offs, old, ou
             codes = keep.tile([P, width], U32, name="w_codes_" + slot, align_bytes=64)
             w_plane = keep.tile([P, width], U8, name="w_plane_" + slot, align_bytes=64)
             nc.vector.quantize_mx(codes[:].bitcast(FP8X4), w_plane[:], grouped[:].rearrange("p m t -> p (m t)"))
-            for place, mt in enumerate(m_tiles):
-                w_codes[side, mt] = codes[:, place * M_TILE : (place + 1) * M_TILE]
-                w_planes[side, mt] = w_plane[:, place * M_TILE : (place + 1) * M_TILE]
+            for index, mt in enumerate(m_tiles):
+                w_codes[side, mt] = codes[:, index * M_TILE : (index + 1) * M_TILE]
+                w_planes[side, mt] = w_plane[:, index * M_TILE : (index + 1) * M_TILE]
 
-        x_planes[0] = keep.tile([P, S], U8, name="x_plane0", align_bytes=64)
-        nc.vector.memset(x_planes[0][:].bitcast(I32), 0)
+        for side in range(2):
+            x_planes[side] = keep.tile([P, S], U8, name="x_plane%d" % side, align_bytes=64)
+            nc.vector.memset(x_planes[side][:].bitcast(I32), 0)
         nc.vector.tensor_copy(picked_scales[0][:], scale_table[:].indirect(lists[0][:]))
-        move_scale_rows(0, range(0, 4))
+        move_scale_rows(0)
         nc.vector.tensor_copy(picked_scales[1][:], scale_table[:].indirect(lists[1][:]))
         quantise_weights(0, [0, 1], "slot_a")
-        load_weights(1, [1], reuse.tile([P, PACK, M_TILE], F32, name="raw_w2_second", align_bytes=64, offset=2048))
 
-        x_planes[1] = reuse.tile([P, S], U8, name="x_plane1", align_bytes=64, offset=0)
-        nc.vector.tensor_copy(x_planes[1][:].bitcast(I32), picked_scales[1][:].bitcast(I32))
-        move_scale_rows(1, range(2, 4))
+        load_weights(1, [1], keep.tile([P, PACK, M_TILE], F32, name="raw_w2_second", tag="scale_table", align_bytes=64))
+        move_scale_rows(1)
 
         gather_words([(0, 0), (0, 1), (1, 0)], "slot_a")
         quantise_weights(1, [0], "slot_b")
         gather_words([(1, 1)], "raw_w2_first")
         quantise_weights(1, [1], "slot_c")
 
-        pieces_out = [(mt, jt) for mt in range(N // M_TILE) for jt in range(S // J_TILE)]
-        acc = {piece: psum.tile([P, J_TILE], F32, name="acc%d_%d" % piece) for piece in pieces_out}
-        by_columns = sorted(pieces_out, key=lambda piece: piece[1])
+        by_rows = [(mt, jt) for mt in range(N // M_TILE) for jt in range(S // J_TILE)]
+        acc = {piece: psum.tile([P, J_TILE], F32, name="acc%d_%d" % piece) for piece in by_rows}
+        by_columns = sorted(by_rows, key=lambda piece: piece[1])
         for side in range(2):
-            for mt, jt in (by_columns, pieces_out)[side]:
+            for mt, jt in (by_columns, by_rows)[side]:
                 nc.tensor.matmul_mx(
                     acc[mt, jt][:],
                     lhsT=w_codes[side, mt].bitcast(FP8X4),
@@ -117,7 +116,7 @@ def tile_picked_phdiff_abs_p_kernel(tc, x_words, x_scales, w1, w2, offs, old, ou
                     start=(side == 0),
                     stop=(side == 1),
                 )
-        for mt, jt in pieces_out:
+        for mt, jt in by_rows:
             result = keep.tile([P, J_TILE], F32, name="result%d_%d" % (mt, jt))
             nc.scalar.activation(result[:], acc[mt, jt][:], ACT.Abs)
             nc.sync.dma_start(out[mt * M_TILE : (mt + 1) * M_TILE, jt * J_TILE : (jt + 1) * J_TILE], result[:])

@@ -51,7 +51,7 @@ def tile_picked_phdiff_abs_p_kernel(tc, x_words, x_scales, w1, w2, offs, old, ou
             nc.sync.dma_start(rows[:], weights[:, :, first : first + width])
             raw[side, m_tiles[0]] = rows
 
-        load_weights(0, [0, 1], keep.tile([P, PACK, N], F32, name="raw_w1", align_bytes=64))
+        load_weights(0, [0, 1], keep.tile([P, PACK, N], F32, name="raw_w1", tag="raw_w1", align_bytes=64))
         nc.sync.dma_start(word_table[:, EARLY:], word_rows[:, EARLY:])
         load_weights(1, [0], keep.tile([P, PACK, M_TILE], F32, name="raw_w2_first", tag="raw_w2_first", align_bytes=64))
 
@@ -88,7 +88,6 @@ def tile_picked_phdiff_abs_p_kernel(tc, x_words, x_scales, w1, w2, offs, old, ou
 
         for side in range(2):
             x_planes[side] = keep.tile([P, S], U8, name="x_plane%d" % side, align_bytes=64)
-            nc.vector.memset(x_planes[side][:].bitcast(I32), 0)
         nc.vector.tensor_copy(picked_scales[0][:], scale_table[:].indirect(lists[0][:]))
         move_scale_rows(0)
         nc.vector.tensor_copy(picked_scales[1][:], scale_table[:].indirect(lists[1][:]))
@@ -97,7 +96,7 @@ def tile_picked_phdiff_abs_p_kernel(tc, x_words, x_scales, w1, w2, offs, old, ou
         load_weights(1, [1], keep.tile([P, PACK, M_TILE], F32, name="raw_w2_second", tag="scale_table", align_bytes=64))
         move_scale_rows(1)
 
-        gather_words([(0, 0), (0, 1), (1, 0)], "slot_a")
+        gather_words([(0, 0), (0, 1), (1, 0)], "raw_w1")
         quantise_weights(1, [0], "slot_b")
         gather_words([(1, 1)], "raw_w2_first")
         quantise_weights(1, [1], "slot_c")

@@ -23,99 +23,104 @@ PLACES = 4
 LINE = 4
 M_TILE = 128
 J_TILE = 256
-EARLY = 384
+EARLY = 448
 
 
 def tile_picked_phdiff_abs_p_kernel(tc, x_words, x_scales, w1, w2, offs, old, out):
     nc = tc.nc
     with ExitStack() as ctx:
         keep = ctx.enter_context(tc.tile_pool(name="keep", bufs=1))
+        shared = ctx.enter_context(tc.tile_pool(name="shared", bufs=1))
         psum = ctx.enter_context(tc.psum_pool(name="psum", bufs=1))
 
+        w1_rows = w1.rearrange("(p t) m -> p t m", t=PACK)
+        w2_rows = w2.rearrange("(p t) m -> p t m", t=PACK)
+        raw_w1 = keep.tile([P, PACK, N], F32, name="raw_w1", tag="raw_w1", align_bytes=64)
+        raw_w2 = keep.tile([P, PACK, M_TILE], F32, name="raw_w2", tag="raw_w2", align_bytes=64)
         lists = [keep.tile([P, S // LIST_ROWS], U16, name="list%d" % side) for side in range(2)]
         word_table = keep.tile([P, T], I32, name="word_table", align_bytes=64)
         word_rows = x_words[0].rearrange("p n t -> p (n t)").bitcast(I32)
         nc.sync.dma_start(word_table[:, :EARLY], word_rows[:, :EARLY])
         nc.sync.dma_start(lists[0][:], offs)
-        nc.sync.dma_start(lists[1][:], old)
 
-        scale_table = keep.tile([P, T], U8, name="scale_table", tag="scale_table", align_bytes=64)
+        scale_table = keep.tile([P, T], U8, name="scale_table", align_bytes=64)
         nc.vector.memset(scale_table[:].bitcast(I32), 0)
         nc.sync.dma_start(scale_table[0:P:BLOCK_ROWS, :].bitcast(I32), x_scales[0].bitcast(I32))
-
-        raw = {}
-
-        def load_weights(side, m_tiles, rows):
-            first, width = m_tiles[0] * M_TILE, len(m_tiles) * M_TILE
-            weights = (w1, w2)[side].rearrange("(p t) m -> p t m", t=PACK)
-            nc.sync.dma_start(rows[:], weights[:, :, first : first + width])
-            raw[side, m_tiles[0]] = rows
-
-        load_weights(0, [0, 1], keep.tile([P, PACK, N], F32, name="raw_w1", tag="raw_w1", align_bytes=64))
+        nc.sync.dma_start(lists[1][:], old)
+        sign = shared.tile([P, 32], F32, name="sign", align_bytes=64, offset=S - 64)
+        nc.vector.memset(sign[:, 0:1], -1.0)
+        nc.sync.dma_start(raw_w1[:], w1_rows)
         nc.sync.dma_start(word_table[:, EARLY:], word_rows[:, EARLY:])
-        load_weights(1, [0], keep.tile([P, PACK, M_TILE], F32, name="raw_w2_first", tag="raw_w2_first", align_bytes=64))
+        nc.sync.dma_start(raw_w2[:], w2_rows[:, :, :M_TILE])
 
         picked_scales = [keep.tile([P, S], U8, name="picked_scales%d" % side, align_bytes=64) for side in range(2)]
         x_planes, picked_words, w_codes, w_planes = {}, {}, {}, {}
 
-        def move_scale_rows(side):
-            for i in range(PLACES):
-                nc.sync.dma_start(
+        def move_scale_rows(queue, side, places):
+            for i in places:
+                queue.dma_start(
                     x_planes[side][i:P:QUADRANT, :].bitcast(I32),
                     picked_scales[side][BLOCK_ROWS * i : P : QUADRANT, :].bitcast(I32),
                 )
 
-        def gather_words(pieces, slot):
-            words = keep.tile([P, len(pieces) * J_TILE], U32, name="picked_" + slot, tag=slot, align_bytes=64)
+        def gather_words(pieces, words):
             for place, (side, jt) in enumerate(pieces):
                 offsets = lists[side][:, jt * J_TILE // LIST_ROWS : (jt + 1) * J_TILE // LIST_ROWS]
                 piece = words[:, place * J_TILE : (place + 1) * J_TILE]
                 nc.vector.tensor_copy(piece, word_table[:].bitcast(U32).indirect(offsets))
                 picked_words[side, jt] = piece
 
-        def quantise_weights(side, m_tiles, slot):
+        def round_rows(grouped, rows, sign):
+            src = rows.rearrange("p t (c n) -> p c t n", n=LINE)
+            dst = grouped.rearrange("p (c n) t -> p c t n", n=LINE)
+            nc.scalar.activation(dst, src, ACT.Copy, scale=sign)
+
+        def quantise(side, m_tiles, grouped):
             width = len(m_tiles) * M_TILE
-            grouped = keep.tile([P, width, PACK], BF16, name="grouped_" + slot, tag=slot, align_bytes=64)
-            src = raw[side, m_tiles[0]][:].rearrange("p t (c n) -> p c t n", n=LINE)
-            dst = grouped[:].rearrange("p (c n) t -> p c t n", n=LINE)
-            nc.scalar.activation(dst, src, ACT.Copy, scale=1.0 if side == 0 else -1.0)
-            codes = keep.tile([P, width], U32, name="w_codes_" + slot, align_bytes=64)
-            w_plane = keep.tile([P, width], U8, name="w_plane_" + slot, align_bytes=64)
+            codes = keep.tile([P, width], U32, name="w_codes%d_%d" % (side, m_tiles[0]), align_bytes=64)
+            w_plane = keep.tile([P, width], U8, name="w_plane%d_%d" % (side, m_tiles[0]), align_bytes=64)
             nc.vector.quantize_mx(codes[:].bitcast(FP8X4), w_plane[:], grouped[:].rearrange("p m t -> p (m t)"))
             for index, mt in enumerate(m_tiles):
                 w_codes[side, mt] = codes[:, index * M_TILE : (index + 1) * M_TILE]
                 w_planes[side, mt] = w_plane[:, index * M_TILE : (index + 1) * M_TILE]
 
-        for side in range(2):
-            x_planes[side] = keep.tile([P, S], U8, name="x_plane%d" % side, align_bytes=64)
+        grouped_w1 = keep.tile([P, N, PACK], BF16, name="grouped_w1", align_bytes=64)
+        round_rows(grouped_w1[:, :M_TILE, :], raw_w1[:, :, :M_TILE], -1.0)
+        round_rows(grouped_w1[:, M_TILE:, :], raw_w1[:, :, M_TILE:], sign[:, 0:1])
         nc.vector.tensor_copy(picked_scales[0][:], scale_table[:].indirect(lists[0][:]))
-        move_scale_rows(0)
+        x_planes[0] = keep.tile([P, S], U8, name="x_plane0", align_bytes=64)
+        move_scale_rows(nc.sync, 0, range(PLACES))
+        nc.sync.dma_start(raw_w1[:, :, :M_TILE], w2_rows[:, :, M_TILE:])
         nc.vector.tensor_copy(picked_scales[1][:], scale_table[:].indirect(lists[1][:]))
-        quantise_weights(0, [0, 1], "slot_a")
+        x_planes[1] = shared.tile([P, S], U8, name="x_plane1", align_bytes=64, offset=0)
+        move_scale_rows(nc.sync, 1, range(PLACES))
+        quantise(0, [0, 1], grouped_w1)
 
-        load_weights(1, [1], keep.tile([P, PACK, M_TILE], F32, name="raw_w2_second", tag="scale_table", align_bytes=64))
-        move_scale_rows(1)
+        gather_words([(0, 0), (0, 1), (1, 0)], shared.tile([P, 3 * J_TILE], U32, name="first_words", align_bytes=64, offset=S))
+        grouped_w2 = [keep.tile([P, M_TILE, PACK], BF16, name="grouped_w2_%d" % mt, tag="grouped_w2_%d" % mt, align_bytes=64) for mt in range(2)]
+        round_rows(grouped_w2[0][:], raw_w2[:], 1.0)
+        round_rows(grouped_w2[1][:], raw_w1[:, :, :M_TILE], 1.0)
+        quantise(1, [0], grouped_w2[0])
+        gather_words([(1, 1)], keep.tile([P, J_TILE], U32, name="last_words", tag="raw_w2", align_bytes=64))
+        quantise(1, [1], grouped_w2[1])
 
-        gather_words([(0, 0), (0, 1), (1, 0)], "raw_w1")
-        quantise_weights(1, [0], "slot_b")
-        gather_words([(1, 1)], "raw_w2_first")
-        quantise_weights(1, [1], "slot_c")
-
-        by_rows = [(mt, jt) for mt in range(N // M_TILE) for jt in range(S // J_TILE)]
-        acc = {piece: psum.tile([P, J_TILE], F32, name="acc%d_%d" % piece) for piece in by_rows}
-        by_columns = sorted(by_rows, key=lambda piece: piece[1])
+        half = J_TILE // 2
+        pieces = [(0, 0, J_TILE), (0, J_TILE, J_TILE), (1, J_TILE, half), (1, 0, J_TILE), (1, J_TILE + half, half)]
+        acc = {piece: psum.tile([P, piece[2]], F32, name="acc%d_%d" % piece[:2]) for piece in pieces}
+        by_columns = sorted(pieces, key=lambda piece: piece[1] // J_TILE)
         for side in range(2):
-            for mt, jt in (by_columns, by_rows)[side]:
+            for mt, first, width in (by_columns, pieces)[side]:
+                jt, inside = divmod(first, J_TILE)
                 nc.tensor.matmul_mx(
-                    acc[mt, jt][:],
+                    acc[mt, first, width][:],
                     lhsT=w_codes[side, mt].bitcast(FP8X4),
                     lhsT_scale=w_planes[side, mt],
-                    rhs=picked_words[side, jt].bitcast(FP8X4),
-                    rhs_scale=x_planes[side][:, jt * J_TILE : (jt + 1) * J_TILE],
+                    rhs=picked_words[side, jt][:, inside : inside + width].bitcast(FP8X4),
+                    rhs_scale=x_planes[side][:, first : first + width],
                     start=(side == 0),
                     stop=(side == 1),
                 )
-        for mt, jt in by_rows:
-            result = keep.tile([P, J_TILE], F32, name="result%d_%d" % (mt, jt))
-            nc.scalar.activation(result[:], acc[mt, jt][:], ACT.Abs)
-            nc.sync.dma_start(out[mt * M_TILE : (mt + 1) * M_TILE, jt * J_TILE : (jt + 1) * J_TILE], result[:])
+        for mt, first, width in pieces:
+            result = keep.tile([P, width], F32, name="result%d_%d" % (mt, first))
+            nc.scalar.activation(result[:], acc[mt, first, width][:], ACT.Abs)
+            nc.sync.dma_start(out[mt * M_TILE : (mt + 1) * M_TILE, first : first + width], result[:])

@@ -24,6 +24,7 @@ LINE = 4
 M_TILE = 128
 J_TILE = 256
 EARLY = 448
+SCALAR_SHARE = 80
 
 
 def tile_picked_phdiff_abs_p_kernel(tc, x_words, x_scales, w1, w2, offs, old, out):
@@ -99,7 +100,15 @@ def tile_picked_phdiff_abs_p_kernel(tc, x_words, x_scales, w1, w2, offs, old, ou
         gather_words([(0, 0), (0, 1), (1, 0)], shared.tile([P, 3 * J_TILE], U32, name="first_words", align_bytes=64, offset=S))
         grouped_w2 = [keep.tile([P, M_TILE, PACK], BF16, name="grouped_w2_%d" % mt, tag="grouped_w2_%d" % mt, align_bytes=64) for mt in range(2)]
         round_rows(grouped_w2[0][:], raw_w2[:], 1.0)
-        round_rows(grouped_w2[1][:], raw_w1[:, :, :M_TILE], 1.0)
+        round_rows(grouped_w2[1][:, :SCALAR_SHARE, :], raw_w1[:, :, :SCALAR_SHARE], 1.0)
+        nc.gpsimd.tensor_scalar(
+            grouped_w2[1][:, SCALAR_SHARE:, :],
+            raw_w1[:, :, SCALAR_SHARE:M_TILE].rearrange("p t m -> p m t"),
+            1.0,
+            0.0,
+            mybir.AluOpType.mult,
+            mybir.AluOpType.add,
+        )
         quantise(1, [0], grouped_w2[0])
         gather_words([(1, 1)], keep.tile([P, J_TILE], U32, name="last_words", tag="raw_w2", align_bytes=64))
         quantise(1, [1], grouped_w2[1])

@@ -23,7 +23,8 @@ PLACES = 4
 LINE = 4
 M_TILE = 128
 J_TILE = 256
-EARLY = 448
+EARLY = 704
+W1_SHARE = 192
 SCALAR_SHARE = 80
 
 
@@ -87,7 +88,15 @@ def tile_picked_phdiff_abs_p_kernel(tc, x_words, x_scales, w1, w2, offs, old, ou
 
         grouped_w1 = keep.tile([P, N, PACK], BF16, name="grouped_w1", align_bytes=64)
         round_rows(grouped_w1[:, :M_TILE, :], raw_w1[:, :, :M_TILE], -1.0)
-        round_rows(grouped_w1[:, M_TILE:, :], raw_w1[:, :, M_TILE:], sign[:, 0:1])
+        round_rows(grouped_w1[:, M_TILE:W1_SHARE, :], raw_w1[:, :, M_TILE:W1_SHARE], sign[:, 0:1])
+        nc.gpsimd.tensor_scalar(
+            grouped_w1[:, W1_SHARE:, :],
+            raw_w1[:, :, W1_SHARE:].rearrange("p t m -> p m t"),
+            sign[:, 0:1],
+            0.0,
+            mybir.AluOpType.mult,
+            mybir.AluOpType.add,
+        )
         nc.vector.tensor_copy(picked_scales[0][:], scale_table[:].indirect(lists[0][:]))
         x_planes[0] = keep.tile([P, S], U8, name="x_plane0", align_bytes=64)
         move_scale_rows(nc.sync, 0, range(PLACES))

@@ -25,6 +25,7 @@ M_TILE = 128
 J_TILE = 256
 EARLY = 704
 W1_SHARE = 192
+FIRST_STEP = 176
 SCALAR_SHARE = 80
 
 
@@ -87,8 +88,8 @@ def tile_picked_phdiff_abs_p_kernel(tc, x_words, x_scales, w1, w2, offs, old, ou
                 w_planes[side, mt] = w_plane[:, index * M_TILE : (index + 1) * M_TILE]
 
         grouped_w1 = keep.tile([P, N, PACK], BF16, name="grouped_w1", align_bytes=64)
-        round_rows(grouped_w1[:, :M_TILE, :], raw_w1[:, :, :M_TILE], -1.0)
-        round_rows(grouped_w1[:, M_TILE:W1_SHARE, :], raw_w1[:, :, M_TILE:W1_SHARE], sign[:, 0:1])
+        round_rows(grouped_w1[:, :FIRST_STEP, :], raw_w1[:, :, :FIRST_STEP], -1.0)
+        round_rows(grouped_w1[:, FIRST_STEP:W1_SHARE, :], raw_w1[:, :, FIRST_STEP:W1_SHARE], sign[:, 0:1])
         nc.gpsimd.tensor_scalar(
             grouped_w1[:, W1_SHARE:, :],
             raw_w1[:, :, W1_SHARE:].rearrange("p t m -> p m t"),

from contextlib import ExitStack

import concourse.mybir as mybir

K, T, S, N = 512, 2048, 512, 256
FLOPS = 2 * 2 * K * N * S

F32 = mybir.dt.float32
BF16 = mybir.dt.bfloat16
I32 = mybir.dt.int32
U32 = mybir.dt.uint32
U16 = mybir.dt.uint16
U8 = mybir.dt.uint8
FP8X4 = mybir.dt.float8_e4m3fn_x4
ACT = mybir.ActivationFunctionType

P = 128
PACK = 4
LIST_ROWS = 16
BLOCK_ROWS = 8
QUADRANT = 32
PLACES = 4
LINE = 4
M_TILE = 128
J_TILE = 256
EARLY = 704
W1_SHARE = 192
FIRST_STEP = 176
SCALAR_SHARE = 80


def tile_picked_phdiff_abs_p_kernel(tc, x_words, x_scales, w1, w2, offs, old, out):
    nc = tc.nc
    with ExitStack() as ctx:
        keep = ctx.enter_context(tc.tile_pool(name="keep", bufs=1))
        shared = ctx.enter_context(tc.tile_pool(name="shared", bufs=1))
        psum = ctx.enter_context(tc.psum_pool(name="psum", bufs=1))

        w1_rows = w1.rearrange("(p t) m -> p t m", t=PACK)
        w2_rows = w2.rearrange("(p t) m -> p t m", t=PACK)
        raw_w1 = keep.tile([P, PACK, N], F32, name="raw_w1", tag="raw_w1", align_bytes=64)
        raw_w2 = keep.tile([P, PACK, M_TILE], F32, name="raw_w2", tag="raw_w2", align_bytes=64)
        lists = [keep.tile([P, S // LIST_ROWS], U16, name="list%d" % side) for side in range(2)]
        word_table = keep.tile([P, T], I32, name="word_table", align_bytes=64)
        word_rows = x_words[0].rearrange("p n t -> p (n t)").bitcast(I32)
        nc.sync.dma_start(word_table[:, :EARLY], word_rows[:, :EARLY])
        nc.sync.dma_start(lists[0][:], offs)

        scale_table = keep.tile([P, T], U8, name="scale_table", align_bytes=64)
        nc.vector.memset(scale_table[:].bitcast(I32), 0)
        nc.sync.dma_start(scale_table[0:P:BLOCK_ROWS, :].bitcast(I32), x_scales[0].bitcast(I32))
        nc.sync.dma_start(lists[1][:], old)
        sign = shared.tile([P, 32], F32, name="sign", align_bytes=64, offset=S - 64)
        nc.vector.memset(sign[:, 0:1], -1.0)
        nc.sync.dma_start(raw_w1[:], w1_rows)
        nc.sync.dma_start(word_table[:, EARLY:], word_rows[:, EARLY:])
        nc.sync.dma_start(raw_w2[:], w2_rows[:, :, :M_TILE])

        picked_scales = [keep.tile([P, S], U8, name="picked_scales%d" % side, align_bytes=64) for side in range(2)]
        x_planes, picked_words, w_codes, w_planes = {}, {}, {}, {}

        def move_scale_rows(queue, side, places):
            for i in places:
                queue.dma_start(
                    x_planes[side][i:P:QUADRANT, :].bitcast(I32),
                    picked_scales[side][BLOCK_ROWS * i : P : QUADRANT, :].bitcast(I32),
                )

        def gather_words(pieces, words):
            for place, (side, jt) in enumerate(pieces):
                offsets = lists[side][:, jt * J_TILE // LIST_ROWS : (jt + 1) * J_TILE // LIST_ROWS]
                piece = words[:, place * J_TILE : (place + 1) * J_TILE]
                nc.vector.tensor_copy(piece, word_table[:].bitcast(U32).indirect(offsets))
                picked_words[side, jt] = piece

        def round_rows(grouped, rows, sign):
            src = rows.rearrange("p t (c n) -> p c t n", n=LINE)
            dst = grouped.rearrange("p (c n) t -> p c t n", n=LINE)
            nc.scalar.activation(dst, src, ACT.Copy, scale=sign)

        def quantise(side, m_tiles, grouped):
            width = len(m_tiles) * M_TILE
            codes = keep.tile([P, width], U32, name="w_codes%d_%d" % (side, m_tiles[0]), align_bytes=64)
            w_plane = keep.tile([P, width], U8, name="w_plane%d_%d" % (side, m_tiles[0]), align_bytes=64)
            nc.vector.quantize_mx(codes[:].bitcast(FP8X4), w_plane[:], grouped[:].rearrange("p m t -> p (m t)"))
            for index, mt in enumerate(m_tiles):
                w_codes[side, mt] = codes[:, index * M_TILE : (index + 1) * M_TILE]
                w_planes[side, mt] = w_plane[:, index * M_TILE : (index + 1) * M_TILE]

        grouped_w1 = keep.tile([P, N, PACK], BF16, name="grouped_w1", align_bytes=64)
        round_rows(grouped_w1[:, :FIRST_STEP, :], raw_w1[:, :, :FIRST_STEP], -1.0)
        round_rows(grouped_w1[:, FIRST_STEP:W1_SHARE, :], raw_w1[:, :, FIRST_STEP:W1_SHARE], sign[:, 0:1])
        nc.gpsimd.tensor_scalar(
            grouped_w1[:, W1_SHARE:, :],
            raw_w1[:, :, W1_SHARE:].rearrange("p t m -> p m t"),
            sign[:, 0:1],
            0.0,
            mybir.AluOpType.mult,
            mybir.AluOpType.add,
        )
        nc.vector.tensor_copy(picked_scales[0][:], scale_table[:].indirect(lists[0][:]))
        x_planes[0] = keep.tile([P, S], U8, name="x_plane0", align_bytes=64)
        move_scale_rows(nc.sync, 0, range(PLACES))
        nc.sync.dma_start(raw_w1[:, :, :M_TILE], w2_rows[:, :, M_TILE:])
        nc.vector.tensor_copy(picked_scales[1][:], scale_table[:].indirect(lists[1][:]))
        x_planes[1] = shared.tile([P, S], U8, name="x_plane1", align_bytes=64, offset=0)
        move_scale_rows(nc.sync, 1, range(PLACES))
        quantise(0, [0, 1], grouped_w1)

        gather_words([(0, 0), (0, 1), (1, 0)], shared.tile([P, 3 * J_TILE], U32, name="first_words", align_bytes=64, offset=S))
        grouped_w2 = [keep.tile([P, M_TILE, PACK], BF16, name="grouped_w2_%d" % mt, tag="grouped_w2_%d" % mt, align_bytes=64) for mt in range(2)]
        round_rows(grouped_w2[0][:], raw_w2[:], 1.0)
        round_rows(grouped_w2[1][:, :SCALAR_SHARE, :], raw_w1[:, :, :SCALAR_SHARE], 1.0)
        nc.gpsimd.tensor_scalar(
            grouped_w2[1][:, SCALAR_SHARE:, :],
            raw_w1[:, :, SCALAR_SHARE:M_TILE].rearrange("p t m -> p m t"),
            1.0,
            0.0,
            mybir.AluOpType.mult,
            mybir.AluOpType.add,
        )
        quantise(1, [0], grouped_w2[0])
        gather_words([(1, 1)], keep.tile([P, J_TILE], U32, name="last_words", tag="raw_w2", align_bytes=64))
        quantise(1, [1], grouped_w2[1])

        half = J_TILE // 2
        pieces = [(0, 0, J_TILE), (0, J_TILE, J_TILE), (1, J_TILE, half), (1, 0, J_TILE), (1, J_TILE + half, half)]
        acc = {piece: psum.tile([P, piece[2]], F32, name="acc%d_%d" % piece[:2]) for piece in pieces}
        by_columns = sorted(pieces, key=lambda piece: piece[1] // J_TILE)
        for side in range(2):
            for mt, first, width in (by_columns, pieces)[side]:
                jt, inside = divmod(first, J_TILE)
                nc.tensor.matmul_mx(
                    acc[mt, first, width][:],
                    lhsT=w_codes[side, mt].bitcast(FP8X4),
                    lhsT_scale=w_planes[side, mt],
                    rhs=picked_words[side, jt][:, inside : inside + width].bitcast(FP8X4),
                    rhs_scale=x_planes[side][:, first : first + width],
                    start=(side == 0),
                    stop=(side == 1),
                )
        for mt, first, width in pieces:
            result = keep.tile([P, width], F32, name="result%d_%d" % (mt, first))
            nc.scalar.activation(result[:], acc[mt, first, width][:], ACT.Abs)
            nc.sync.dma_start(out[mt * M_TILE : (mt + 1) * M_TILE, first : first + width], result[:])
